import numpy as np, ml_dtypes
CORES = [36,164,52,180,100,228,116,244]
N = 8
BF = ml_dtypes.bfloat16
W, S, RO, LIM = 2048, 128, 4, 4
HEARER = [[4, 5, 6, 7, 0, 1, 2, 3], [1, 2, 3, 4, 5, 6, 7, 0], [3, 4, 5, 6, 7, 0, 1, 2], [6, 7, 0, 1, 2, 3, 4, 5]]
def world(rng, skew):
    m = rng.integers(2, 5, (8, 1, 1)); pn = rng.integers(2, 9, (1, 8, 1)); noise = 0.05 + 0.45 * rng.random((N, 8, 1, 1))
    alph = np.argsort(rng.random((8, 16, 513)), axis=-1)[..., :4] - 256
    proto = (rng.random((8, 8, 16)) * m).astype(np.int64); z = (rng.random((N, 8, W)) * pn).astype(np.int64)
    e = proto[np.arange(8)[None, :, None], z]
    u = (rng.random(e.shape, dtype=np.float32) ** skew * m).astype(np.int64)
    e = np.where(rng.random(e.shape, dtype=np.float32) < noise, np.minimum(u, 3), e)
    return np.ascontiguousarray(alph[np.arange(8)[None, :, None, None], np.arange(16), e].transpose(0, 1, 3, 2))
def parts(rng, skew=1):
    X = world(rng, skew)
    As = np.minimum((W * rng.random((N, 8, 16, W)) ** skew).astype(np.int64), W - 1)
    C = np.minimum((W * rng.random((N, 8, 16, S)) ** skew).astype(np.int64), W - 1); H = np.minimum((W * rng.random((N, 8, 16, S)) ** skew).astype(np.int64), W - 1)
    R = np.argsort(rng.random((N, 8, 16, S)), axis=2); A = np.minimum((256 * rng.random((N, 8, S)) ** skew).astype(np.int64), 255)
    return X, As, C, H, R, A
def pack(X, As, C, H, R, A):
    return {"x": np.ascontiguousarray(X.reshape(N, 128, W)).astype(np.float32).astype(BF), "assoc": np.ascontiguousarray(As.reshape(N, 128, W)).astype(np.int32),
            "ctx": np.ascontiguousarray(C.reshape(N, 128, S)).astype(np.int32), "cand": np.ascontiguousarray(H.reshape(N, 128, S)).astype(np.int32),
            "pref": np.ascontiguousarray(R.reshape(N, 128, S)).astype(np.int32), "fail0": np.ascontiguousarray(A).astype(np.int32)}
def setup_inputs(rng):
    return pack(*parts(rng))
def setup_inputs_spread(rng):
    X, As, C, H, R, A = parts(rng, 3)
    X = np.where((X == X[0, :, :, :1]) & (rng.random((8, 16, 1)) < 0.5), 0, X)
    share = 0.05 + 0.4 * rng.random((N, 8, 1, 1))
    X = np.where(rng.random((N, 8, 1, W)) < share, rng.integers(-256, 257, X.shape), X)
    X = np.where((X == 0) & (rng.random(X.shape, dtype=np.float32) < 0.5), -0.0, X)
    return pack(X, As, C, H, R, A)
def endlist(rng, shape):
    return np.where(rng.random(shape) < 0.68, rng.choice(np.array([0, W - 1]), shape), rng.integers(0, W, shape))
def setup_inputs_ends(rng):
    proto = rng.choice(np.array([-1, 1]), (8, 6, 16)); e = proto[np.arange(8)[None, :, None], rng.integers(0, 6, (N, 8, W))]
    e = np.where(rng.random(e.shape, dtype=np.float32) < 0.05 + 0.3 * rng.random((N, 8, 1, 1)), -e, e)
    u = rng.random((N, 8, W, 1)); e = np.where(u < 0.15, 1, np.where(u < 0.3, -1, e))
    X = np.ascontiguousarray(256 * e.transpose(0, 1, 3, 2)); sg = 256 * rng.choice(np.array([-1, 1]), (8, 1)); a = np.arange(16)[:, None]
    X[..., 0] = -sg; X[..., W - 1] = sg
    X[..., W - 16:W - 1] = sg[:, :, None] * np.where(np.arange(16)[:, None] == np.arange(1, 16), -1, 1)
    X[..., 1:16] = -X[..., W - 16:W - 1]
    X[..., 16:32] = sg[:, :, None] * np.where((a >= 1) & (a <= np.arange(16)), 1, -1)
    As = endlist(rng, (N, 8, 16, W)); C = endlist(rng, (N, 8, 16, S)); H = endlist(rng, (N, 8, 16, S))
    C[..., S - 8:] = np.concatenate([np.array([W - 1]), np.arange(W - 16, W - 1)])[:, None]
    H[..., S - 3:] = 0; H[:, :, 15, S - 1] = W - 1; H[:, :, 14:, S - 3] = W - 1
    C[..., S - 4] = a[:, 0]; H[..., S - 4] = W - 1
    H[..., S - 8:S - 4] = 31 - np.arange(11, 15) - (a < rng.integers(1, 16, (N, 8, 1, 4)))
    C[..., 0] = W - 1; C[:, :, 0, 0] = 0; H[..., 0] = W - 1
    C[..., 1] = W - 1; H[..., 1] = 0
    R = np.where(rng.random((N, 8, 1, S)) < 0.5, a, 15 - a); R = np.where(rng.random((N, 8, 1, S)) < 0.25, np.argsort(rng.random((N, 8, 16, S)), axis=2), R)
    return pack(X, As, C, H, R, rng.choice(np.array([0, 255]), (N, 8, S)))
def setup_inputs_corners(rng):
    X, As, C, H, R, A = parts(rng); k = np.arange(16); kk = k[:, None]; o = np.arange(1, S, 2); M = len(o); sp = np.argsort(np.array(HEARER[0]))
    A = rng.choice(np.array([0, 1, 2, 3, 252, 253, 254, 255]), (N, 8, S))
    R = np.where(rng.random((N, 8, 1, S)) < 0.3, np.where(rng.random((N, 8, 1, S)) < 0.5, kk, 15 - kk), R)
    rk = R[..., o].transpose(0, 1, 3, 2)[:, :, :, None, :]
    kind = rng.integers(0, 4, (N, 8, M, 1, 1)); b = rng.integers(-256, 256, (N, 8, M, 1, 16))
    one = (rk == kk) | ((rk > kk) & (rng.random((N, 8, M, 16, 16)) < 0.5))
    dx = (((kind == 1) & one) | (kind == 2) | ((kind == 3) & (rk == 15) & (kk >= 8))) & (kk > 0)
    room = (LIM + (A[..., o] & 3))[..., None, None]; how = rng.integers(0, 4, (N, 8, M, 1, 1))
    m = np.where(how == 0, 0, np.where(how == 1, room, np.where(how == 2, room + 1, 16)))
    w = np.where(kind == 0, 0, rng.choice(np.array([0, 1, 14, 15]), (N, 8, M, 1, 1)))
    dy = np.where(kind == 3, rk < m, rk >= 16 - m) | (kk < w)
    cols = (16 * o[:, None] + k).reshape(-1)
    X[..., cols] = (b + dx).transpose(0, 1, 4, 2, 3).reshape(N, 8, 16, 16 * M)
    X[..., cols - 16] = (b + dy).transpose(0, 1, 4, 2, 3).reshape(N, 8, 16, 16 * M)[sp]
    C[..., o] = 16 * o + kk; H[..., o] = 16 * (o - 1) + kk
    C[:, 6, :, 0::2] = C[:, 6, :1, 0::2]; H[:, 2, :, 0::2] = H[:, 2, :1, 0::2]
    As[:, 3] = np.where(rng.random((N, 16, W)) < 0.5, np.arange(W), As[:, 3]); As[:, 5] = rng.choice(np.array([0, W - 1]), (N, 16, W))
    return pack(X, As, C, H, R, A)
def setup_inputs_bulk(rng):
    X, As, C, H, R, A = parts(rng); h = W // 2; v = h // 2; m = min(LIM, 8)
    ga, gb, gc, gd, ge = [int(i) for i in rng.permutation(8)[:5]]
    X[:, ga, :, :h] = 2 * rng.integers(-128, 129, (N, 16, h)); X[:, gb, :, :h] = 2 * rng.integers(-128, 129, (16, 1))
    for g in (ga, gb):
        X[:, g, :, h:] = 2 * rng.integers(-128, 128, (N, 16, W - h)) + 1
        C[:, g] = rng.integers(h, W, (N, 16, S)); C[:, g, 0] = rng.integers(0, h, (N, S))
    H[:, ga] = rng.integers(h, W, (N, 16, S)); H[:, gb] = rng.integers(0, h, (N, 16, S))
    X[:, gc] = (np.argsort(rng.random((16, 513)), axis=-1)[:, :N] - 256).T[:, :, None]; A[:, gc, ::2] = 255
    X[:, gd] = 2 * rng.integers(-128, 128, (16, 1))
    X[:, gd, 8:8 + m, v:h] += rng.integers(0, 2, (N, m, h - v)); X[:, gd, :8, h:] += rng.integers(0, 2, (N, 8, W - h))
    C[:, gd] = rng.integers(h, W, (N, 16, S)); C[:, gd, 0] = rng.integers(0, v, (N, S)); H[:, gd] = rng.integers(v, h, (N, 16, S))
    near = LIM + ((254 + RO) & 3); b = 2 * rng.integers(-128, 128, (16, 1))
    X[:, ge, :, :h] = b; X[:, ge, :, h:] = b + 1; X[:, ge, :, h + v:] = b + (np.argsort(rng.random(16)) < near)[:, None]; X[:, ge, :, ::16] = b
    C[:, ge] = h + 2 * rng.integers(0, v // 2, (N, 16, S)) + 1
    H[:, ge] = N * rng.integers(0, h // N, (N, 16, S)) + np.arange(N)[:, None, None]
    As[:, ge, 0, :h] = h + v * (np.arange(h) % N == np.array(HEARER[RO - 2])[:, None]) + 2 * rng.integers(0, v // 2, (N, h)) + 1
    A[:, ge, ::2] = 255
    return pack(X, As, C, H, R, A)
def check_inputs(d):
    bad = []
    for name, lo, hi in (("x", -256, 256), ("assoc", 0, W - 1), ("ctx", 0, W - 1), ("cand", 0, W - 1), ("pref", 0, 15), ("fail0", 0, 255)):
        v = np.asarray(d[name]).astype(np.float64)
        if not (np.min(v) >= lo and np.max(v) <= hi): bad.append("range of " + name)
        if np.any(v != np.rint(v)): bad.append("whole numbers in " + name)
    if np.any(np.sort(np.asarray(d["pref"]).astype(np.int64).reshape(-1, 8, 16, S), axis=2) != np.arange(16)[:, None]): bad.append("permutations in pref")
    return bad
def pick(a, ix):
    return np.take_along_axis(a, ix.reshape(N, 8, 1, 16 * S), 3).reshape(N, 8, 16, 16, S)
def front(R, row, fail):
    old = np.take_along_axis(R, row[:, :, None, :], 2)
    moved = np.where(np.arange(16)[:, None] == row[:, :, None, :], 0, R + (R < old))
    return np.where(fail[:, :, None, :], moved, R)
def reference(x, assoc, ctx, cand, pref, fail0):
    X = x.astype(np.float32).astype(np.int16).reshape(N, 8, 16, W); As = assoc.astype(np.int64).reshape(N, 8, 16, W)
    C = ctx.astype(np.int64).reshape(N, 8, 16, S); H = cand.astype(np.int64).reshape(N, 8, 16, S); R = pref.astype(np.int64).reshape(N, 8, 16, S); A = fail0.astype(np.int64).reshape(N, 8, S)
    for t in range(RO):
        q = np.array(HEARER[t]); sp = np.argsort(q)
        xk = pick(X, C); x0 = xk[:, :, :, 0]
        first = np.min(np.where(xk != x0[:, :, :, None], R[:, :, :, None], 16), axis=2)
        desc = np.any(R[:, :, :, None] == first[:, :, None], axis=3)
        top = np.min(first, axis=2)
        yk = pick(X, H)[q]
        miss = np.sum((yk != x0[:, :, :, None]) & desc[:, :, :, None], axis=2)
        ks = np.argmin(miss, axis=2)
        n = np.take_along_axis(H[q], ks[:, :, None, :], 2)[:, :, 0]
        y = np.take_along_axis(yk, ks[:, :, None, None, :], 3)[:, :, :, 0]
        un = y != x0; fail = np.sum(un, axis=2) > LIM + (A & 3); row = np.argmin(np.where(un, R, 16), axis=2)
        A = A + fail
        R = front(R, row, fail); R = front(R, row[sp], fail[sp])
        cn = np.take_along_axis(As, n[:, :, None, :], 3); hn = np.take_along_axis(As, n[sp][:, :, None, :], 3)
        C = np.where((first == top[:, :, None]) & (first < 16), cn, C); C[:, :, 0] = cn[:, :, 0]
        H = np.where(miss[sp] > 0, hn, H)
        if t < RO - 1:
            put = np.broadcast_to((16 * np.arange(S) + ks[sp])[:, :, None, :], (N, 8, 16, S))
            np.put_along_axis(X, put, np.where(desc, x0, y)[sp], 3)
    return {"yctx": C.reshape(N, 128, S).astype(np.float32), "ycand": H.reshape(N, 128, S).astype(np.float32), "ypref": R.reshape(N, 128, S).astype(np.float32), "yfail": A.astype(np.float32)}

@@ -1,0 +1,393 @@
+import math
+from concourse.mybir import AluOpType, ActivationFunctionType
+
+ADD, SUB, MUL, MAX, MIN = AluOpType.add, AluOpType.subtract, AluOpType.mult, AluOpType.max, AluOpType.min
+GT, LT, LE, EQ, NE = AluOpType.is_gt, AluOpType.is_lt, AluOpType.is_le, AluOpType.is_equal, AluOpType.not_equal
+SHR, AND = AluOpType.logical_shift_right, AluOpType.bitwise_and
+AF = ActivationFunctionType
+LN2 = math.log(2.0)
+STEP = (4, 1, 3, 6)
+RO = 4
+B16, F32, I32, U16, F16 = "bfloat16", "float32", "int32", "uint16", "float16"
+
+SCRATCH = {}
+for _n, _c, _d in (
+        ("X", 2048, B16), ("As", 2048, I32), ("XG", 2048, B16), ("YG", 2048, B16), ("Z", 2048, B16), ("RL", 2048, B16),
+        ("NQ", 2048, B16), ("SEL", 2048, B16), ("SELh", 2048, F16), ("SELT", 2048, B16),
+        ("ctxi", 128, I32), ("candi", 128, I32), ("prefi", 128, I32), ("fi", 128, I32), ("ff", 128, F32), ("E8", 128, F32),
+        ("Rf", 128, F32), ("Cf", 128, F32), ("Hf", 128, F32), ("Cu", 128, U16), ("Hu", 128, U16), ("Ai", 128, I32),
+        ("Am", 128, I32), ("Af", 128, F32), ("W4", 512, B16), ("X4", 512, B16), ("w32", 128, B16), ("pre", 128, B16),
+        ("pci", 8, I32), ("pgi", 8, I32), ("pki", 8, I32), ("pcf", 8, F32), ("pgf", 8, F32), ("pkf", 8, F32), ("nk0", 8, F32),
+        ("biask", 8, F32), ("pk16", 8, F32), ("i8", 8, F32), ("i16", 16, F32), ("KJ", 16, F32), ("base", 8, B16),
+        ("rowi", 128, F32), ("rowg", 128, F32), ("ID", 128, B16), ("NI", 128, B16), ("BLK", 128, B16), ("HB", 128, B16),
+        ("NB", 128, B16), ("B6", 128, B16), ("GM", 128, B16), ("TM", 128, B16), ("JM", 128, B16), ("ACM", 128, B16),
+        ("C512", 128, B16), ("Vb", 128, B16), ("nm", 128, F32), ("mm", 128, F32), ("Cm", 128, F32), ("T1", 128, F32),
+        ("T2", 128, F32), ("nh", 128, F32), ("hh", 128, F32), ("Hm", 128, F32), ("und", 128, B16), ("dsc", 128, B16),
+        ("dx", 128, B16), ("EE", 128, B16), ("OH", 128, B16), ("HOH", 128, F16), ("KOH", 128, B16), ("SL", 8, U16),
+        ("UN", 128, B16), ("UW", 128, B16), ("TT", 128, B16), ("NF", 128, B16), ("Fb", 128, B16),
+        ("e2", 128, F32), ("nF2", 128, F32), ("DD", 128, F32), ("R4", 128, F32), ("R2", 128, F32), ("qq", 128, B16),
+        ("bb", 128, F32), ("tq", 128, F32), ("Ro", 128, F32)):
+    SCRATCH[_n] = ("sbuf", [128, _c], _d)
+for _t in range(RO):
+    for _n, _c, _d in (("MW", 256, B16), ("MX", 256, B16), ("NL", 8, U16), ("FS", 128, B16)):
+        SCRATCH["%ss%d" % (_n, _t)] = ("sbuf", [128, _c], _d)
+        SCRATCH["%sr%d" % (_n, _t)] = ("sbuf", [128, _c], _d)
+BANKS = ["PA0", "PA1", "PA2", "PA3", "PB0", "PB1", "PC", "PD"]
+for _n in BANKS:
+    SCRATCH[_n] = ("psum", [128, 512], "float32")
+KINDS = ["MW", "MX", "NL", "FS"]
+SEMAPHORES = ["qV", "qS", "qP", "qG", "sent"] + ["d%d" % _i for _i in range(12)] + \
+             ["a%s%d" % (_k, _t) for _k in KINDS for _t in range(RO)]
+
+
+def rank_program(g, core, T, topo):
+    rank = T.rank_of(core)
+    if rank is None:
+        return
+    n_ranks = len(T.cores)
+    queue = {"V": g.vector, "S": g.scalar, "P": g.tensor, "G": g, "Y": g.sync}
+    known = {q: {} for q in queue}
+    total = {}
+    acc = {}
+    count = [0, 0]
+
+    def need(q, recs):
+        for idx, sem, val, clock in sorted(recs, key=lambda r: -r[0]):
+            if known[q].get(sem, 0) >= val:
+                continue
+            queue[q].wait_ge(T.sem[sem], val)
+            for s, v in clock.items():
+                if known[q].get(s, 0) < v:
+                    known[q][s] = v
+
+    def note(name, c0, c1, write, sem, val, clock):
+        acc.setdefault(name, {})[(sem, c0, c1, write)] = (count[0], val, clock)
+
+    def op(q, call, reads, writes, sem=None, inc=1):
+        own = "q" + q
+        recs = []
+        for keys, w in ((reads, False), (writes, True)):
+            for name, c0, c1 in keys:
+                bank = name in BANKS
+                for (s, a, b, wr), (idx, val, clock) in acc.get(name, {}).items():
+                    if not bank and (b <= c0 or c1 <= a):
+                        continue
+                    if s == own:
+                        if (w and q == "P") or not wr or (bank and (b <= c0 or c1 <= a)):
+                            continue
+                    elif not bank and not w and not wr:
+                        continue
+                    recs.append((idx, s, val, clock))
+        need(q, recs)
+        sem = sem or own
+        total[sem] = total.get(sem, 0) + inc
+        call().then_inc(T.sem[sem], inc)
+        count[0] += 1
+        clock = dict(known[q])
+        clock[sem] = total[sem]
+        for name, c0, c1 in reads:
+            note(name, c0, c1, False, sem, total[sem], clock)
+        for name, c0, c1 in writes:
+            note(name, c0, c1, True, sem, total[sem], clock)
+
+    def b(name, c0=0, c1=None, st=1, p=128):
+        if c1 is None:
+            c1 = SCRATCH[name][1][1] if c0 == 0 else c0 + 128
+        ap = T[name][0:p, c0:c1] if st == 1 else T[name][0:p, c0:c1:st]
+        return ap, [(name, c0, c1)]
+
+    def col(name, j=0, p=128):
+        return T[name][0:p, j:j + 1], [(name, j, j + 1)]
+
+    def ind(win, offs):
+        return win[0].indirect(offs[0]), win[1] + offs[1]
+
+    def tt(out, i0, i1, o):
+        op("V", lambda: g.vector.tensor_tensor(out[0], i0[0], i1[0], o), i0[1] + i1[1], out[1])
+
+    def ts(out, i0, s1, o0, s2=None, o1=None):
+        keys = list(i0[1])
+        v = []
+        for s in (s1, s2):
+            if isinstance(s, tuple):
+                keys += s[1]
+                v.append(s[0])
+            else:
+                v.append(s)
+        if o1 is None:
+            op("V", lambda: g.vector.tensor_scalar(out[0], i0[0], v[0], None, o0), keys, out[1])
+        else:
+            op("V", lambda: g.vector.tensor_scalar(out[0], i0[0], v[0], v[1], o0, o1), keys, out[1])
+
+    def cp(out, i0):
+        op("V", lambda: g.vector.tensor_copy(out[0], i0[0]), i0[1], out[1])
+
+    def fill(out, v):
+        op("V", lambda: g.vector.memset(out[0], v), [], out[1])
+
+    def act(out, i0, f, scale=1.0, bias=None):
+        keys = list(i0[1])
+        sc = scale
+        if isinstance(scale, tuple):
+            keys += scale[1]
+            sc = scale[0]
+        if bias is None:
+            op("S", lambda: g.scalar.activation(out[0], i0[0], f, scale=sc), keys, out[1])
+        else:
+            op("S", lambda: g.scalar.activation(out[0], i0[0], f, bias=bias[0], scale=sc), keys + bias[1], out[1])
+
+    def mm(out, lt, rh, start=True, stop=True):
+        op("P", lambda: g.tensor.matmul(out[0], lt[0], rh[0], start, stop), lt[1] + rh[1], out[1])
+
+    def dma(q, out, i0, reads, writes):
+        s = "d%d" % count[1]
+        count[1] += 1
+        op(q, lambda: queue[q].dma_start(out, i0), reads, writes, s, 16)
+
+    def send(kind, t, dst_rank, src_rank):
+        dst = T.cores[dst_rank]
+        s, r, name = "%ss%d" % (kind, t), "%sr%d" % (kind, t), "a%s%d" % (kind, t)
+        recs = [(i, sm, v, c) for (sm, a, e, wr), (i, v, c) in acc.get(s, {}).items() if wr]
+        need("G", recs)
+        rid, pid = topo.addr(dst, core)
+        ne = len(topo.engines(core, dst))
+        g.remote_dma(out_ap=T[r][:], in_ap=T[s][:], remote_sem=T.sem[name], local_sem=T.sem["sent"], pid=pid, routing_id=rid,
+                     dma_engine_mask=topo.mask(core, dst))
+        total["sent"] = total.get("sent", 0) + ne
+        src = T.cores[src_rank]
+        arrive = len(topo.engines(src, core))
+        total[name] = arrive
+        count[0] += 1
+        note(r, 0, SCRATCH[r][1][1], True, name, arrive, {name: arrive})
+
+    def sel(name, k):
+        return b(name, 128 * k, 128 * k + 128)
+
+    def load(q, name, src, p=128):
+        dma(q, T[name][0:p, :], src, [], [(name, 0, SCRATCH[name][1][1])])
+
+    load("S", "prefi", T.pref[:])
+    load("S", "ctxi", T.ctx[:])
+    load("Y", "X", T.x[:])
+    load("Y", "fi", T.fail0[:], 8)
+    load("Y", "candi", T.cand[:])
+    load("Y", "As", T.assoc[:])
+
+    def iota(out, pat, base, cm, flag=True):
+        op("G", lambda: g.iota(out[0], pat, base, cm, allow_small_or_imprecise_dtypes=flag), [], out[1])
+
+    iota(b("pci", 0, 1), [[0, 1]], 0, 1, False)
+    iota(b("rowi"), [[1, 128]], 0, 0)
+    iota(b("rowg"), [[1, 8], [0, 16]], 0, 0)
+    iota(b("i8"), [[256, 8]], 0, 0)
+    iota(b("i16"), [[1, 16]], 0, 0)
+
+    ts(b("pgi", 0, 1), b("pci", 0, 1), 4, SHR)
+    ts(b("pki", 0, 1), b("pci", 0, 1), 15, AND)
+    cp(b("pcf", 0, 1), b("pci", 0, 1))
+    cp(b("pgf", 0, 1), b("pgi", 0, 1))
+    cp(b("pkf", 0, 1), b("pki", 0, 1))
+    cp(b("Rf"), b("prefi"))
+    act(b("MWs0", 0, 128), b("Rf"), AF.Exp, scale=-5.0 * LN2)
+    cp(b("Cu"), b("ctxi"))
+    ts(b("ID"), b("rowi"), col("pcf"), EQ)
+    ts(b("NI"), b("rowi"), col("pcf"), EQ, -1.0, MUL)
+    ts(b("HB"), b("rowg"), col("pgf"), EQ, 0.5, MUL)
+    ts(b("BLK"), b("rowg"), col("pgf"), EQ)
+    tt(b("GM"), b("ID"), b("HB"), SUB)
+    ts(b("ACM"), b("NI"), float(2.0 ** 47), MUL)
+    fill(b("C512"), 512.0)
+    for j in range(4):
+        cp(b("W4", 128 * j, 128 * j + 128), b("MWs0", 0, 128))
+    ts(b("E8", 0, 128, 1, 8), b("rowg", 0, 128, 1, 8), col("pcf", 0, 8), EQ)
+    cp(b("ff", 0, 128, 1, 8), b("fi", 0, 128, 1, 8))
+    mm(b("PC", 0, 128), b("E8", 0, 128, 1, 8), b("ff", 0, 128, 1, 8))
+    cp(b("Ai"), b("PC", 0, 128))
+    ts(b("Am"), b("Ai"), 3, AND)
+    ts(b("MWs0", 128, 256), b("Am"), 4, ADD)
+    cp(b("Cf"), b("ctxi"))
+
+    def constants_late():
+        ts(b("B6"), b("BLK"), 0.0625, MUL)
+        tt(b("TM"), b("ID"), b("B6"), SUB)
+        ts(b("NB"), b("BLK"), -1.0, MUL)
+        ts(b("JM"), b("GM"), 0.015625, MUL)
+        ts(b("nk0", 0, 1), b("pkf", 0, 1), 0.0, NE)
+        ts(b("biask", 0, 1), b("pkf", 0, 1), -LN2, MUL, 120.0 * LN2, ADD)
+        ts(b("pk16", 0, 1), b("pkf", 0, 1), 16.0, MUL)
+        ts(b("base"), b("i8"), col("pk16"), ADD)
+        ts(b("KJ"), b("i16"), col("pkf"), EQ)
+        cp(b("Hu"), b("candi"))
+        cp(b("Hf"), b("candi"))
+
+    def selectors():
+        fill(b("SEL"), 0.0)
+        for gg in range(8):
+            cp((T.SEL[:, 16 * gg:16 * gg + 129 * 15 + 1:129], [("SEL", 0, 2048)]), b("BLK", 16 * gg, 16 * gg + 16))
+        cp(b("SELh"), b("SEL"))
+
+    def gather(q, dst, offs, s0, s1):
+        out = b(dst, 16 * s0, 16 * s1)
+        src = ind(b("X"), b(offs, s0, s1))
+        if q == "V":
+            cp(out, src)
+        else:
+            act(out, src, AF.Copy)
+
+    for t in range(RO):
+        q_rank, s_rank = (rank + STEP[t]) % n_ranks, (rank - STEP[t]) % n_ranks
+        MWs, MWr, MXs, MXr = "MWs%d" % t, "MWr%d" % t, "MXs%d" % t, "MXr%d" % t
+        NLs, NLr, FSs, FSr = "NLs%d" % t, "NLr%d" % t, "FSs%d" % t, "FSr%d" % t
+        last = t == RO - 1
+
+        gather("V", "XG", "Cu", 0, 32)
+        gather("S", "XG", "Cu", 32, 64)
+        gather("V", "XG", "Cu", 64, 96)
+        gather("S", "XG", "Cu", 96, 128)
+        for h in range(2):
+            for k in range(1, 16):
+                o = b("PA%d" % ((k - 1) // 4), (k - 1) % 4 * 128 + 64 * h, (k - 1) % 4 * 128 + 64 * h + 64)
+                mm(o, b("ID"), b("XG", 1024 * h + k, 1024 * h + 1024, 16), True, False)
+                mm(o, b("NI"), b("XG", 1024 * h, 1024 * h + 1024, 16), False, True)
+        if t:
+            tt(b(MWs, 0, 128), b("pre"), b("FSr%d" % (t - 1)), MAX)
+            for j in range(4):
+                cp(b("W4", 128 * j, 128 * j + 128), b(MWs, 0, 128))
+        cp(b(MXs, 128, 256), b("XG", 0, 2048, 16))
+        if t:
+            mm(b("PC", 0, 128), b("BLK"), b("FSr%d" % (t - 1)))
+            tt(b("Ai"), b("PC", 0, 128), b("Ai"), ADD)
+            ts(b("Am"), b("Ai"), 3, AND)
+            ts(b(MWs, 128, 256), b("Am"), 4, ADD)
+        send("MW", t, q_rank, s_rank)
+        width = (512, 512, 512, 384)
+        dbank = ("PB0", "PB1", "PA0", "PA1")
+        for i in range(4):
+            n = width[i]
+            act(b("PA%d" % i, 0, n), b("PA%d" % i, 0, n), AF.Abs, scale=64.0)
+        for i in range(4):
+            n = width[i]
+            tt(b("Z", 512 * i, 512 * i + n), b("PA%d" % i, 0, n), b("W4", 0, n), MIN)
+            mm(b(dbank[i], 0, n), b("GM"), b("Z", 512 * i, 512 * i + n))
+        for i in range(4):
+            n = width[i]
+            if i < 2:
+                act(b("RL", 512 * i, 512 * i + n), b(dbank[i], 0, n), AF.Relu, scale=float(2.0 ** 70))
+            else:
+                ts(b("RL", 512 * i, 512 * i + n), b(dbank[i], 0, n), 0.0, MAX, float(2.0 ** 70), MUL)
+        mm(b("PC", 0, 128), b("ID"), b("C512"), True, False)
+        for k in range(15):
+            mm(b("PC", 0, 128), b("ACM"), b("RL", 128 * k, 128 * k + 128), False, k == 14)
+        tt(b(MXs, 0, 128), b("PC", 0, 128), b(MXs, 128, 256), MAX)
+        send("MX", t, q_rank, s_rank)
+
+        if t == 0:
+            constants_late()
+            gather("S", "YG", "Hu", 0, 64)
+        gather("S", "YG", "Hu", 96, 128)
+        gather("V", "YG", "Hu", 64, 96)
+        if t == 0:
+            selectors()
+        for k in range(16):
+            mm(b("PA%d" % (k // 4), k % 4 * 128, k % 4 * 128 + 128), b("ID"), b("YG", k, 2048, 16))
+        for k in range(1, 16):
+            mm(b("PD", 0, 128), sel("SEL", k), b("Z", 128 * (k - 1), 128 * k), k == 1, k == 15)
+        cp(b("Vb"), b("PD", 0, 128))
+        mm(b("PB0", 0, 128), b("TM"), b("Vb"))
+        ts(b("w32"), b(MWs, 0, 128), float(2.0 ** -10), MUL)
+        ts(b("nm"), b("PB0", 0, 128), 0.0, LE, col("nk0"), MUL)
+        ts(b("mm"), b("nm"), -1.0, MUL, 1.0, ADD)
+        tt(b("Cm"), b("Cf"), b("nm"), MUL)
+        if t < 3:
+            for j in range(6 * t, min(16, 6 * t + 6)):
+                act(sel("SELT", j), b("BLK"), AF.Copy, scale=col("KJ", j))
+
+        for j in range(4):
+            act(b("X4", 128 * j, 128 * j + 128), b(MXr, 0, 128), AF.Copy)
+        for k in range(4):
+            tt(b("NQ", 128 * k, 128 * k + 128), b("PA0", 128 * k, 128 * k + 128), b(MXr, 0, 128), NE)
+        ts(b("und"), b(MXr, 0, 128), 512.0, EQ)
+        mm(b("PC", 0, 128), b("NB"), b("und"), True, False)
+        for i in range(1, 4):
+            tt(b("NQ", 512 * i, 512 * i + 512), b("PA%d" % i), b("X4"), NE)
+        for k in range(16):
+            mm(b("PC", 0, 128), sel("SEL", k), b("NQ", 128 * k, 128 * k + 128), False, k == 15)
+        act(b("EE"), b("PC", 0, 128), AF.Exp, scale=-16.0 * LN2, bias=col("biask"))
+        mm(b("PD", 0, 128), b("HB"), b("EE"))
+        if not last:
+            ts(b("dsc"), b(MXr, 0, 128), 512.0, NE)
+            tt(b("dx"), b(MXr, 128, 256), b("dsc"), MUL)
+        tt(b("OH"), b("EE"), b("PD", 0, 128), GT)
+        tt(b("HOH"), b("OH"), b("Hf"), MUL)
+        for a in range(16):
+            mm(b("PB0", 0, 8), sel("SELh", a), b("HOH", a, 128, 16), a == 0, a == 15)
+        if not last:
+            act(b("KOH"), b("OH"), AF.Copy, scale=col("pkf"))
+            mm(b("PB1", 0, 8), b("ID"), b("base"), True, False)
+            for a in range(16):
+                mm(b("PB1", 0, 8), sel("SEL", a), b("KOH", a, 128, 16), False, a == 15)
+        ts(b("nh"), b("PC", 0, 128), 0.0, LE)
+        ts(b("hh"), b("PC", 0, 128), 0.0, GT)
+        cp(b(NLs), b("PB0", 0, 8))
+        send("NL", t, s_rank, q_rank)
+
+        tt(b("UN"), ind(b("X"), b(NLs)), b(MXr, 128, 256), NE)
+        mm(b("PA0", 0, 128), b("BLK"), b("UN"))
+        tt(b("UW"), b("UN"), b(MWr, 0, 128), MUL)
+        mm(b("PA1", 0, 128), b("JM"), b("UW"))
+        if not last:
+            tt(b("TT"), ind(b("X"), b(NLs)), b("und"), MUL)
+        tt(b("NF"), b("PA0", 0, 128), b(MWr, 128, 256), LE)
+        tt(b(FSs), b("PA1", 0, 128), b("NF"), GT)
+        send("FS", t, s_rank, q_rank)
+        if not last:
+            cp(b("SL"), b("PB1", 0, 8))
+            win = ind(b("X"), b("SL"))
+            op("V", lambda: g.vector.tensor_tensor(win[0], T.TT[:], T.dx[:], ADD),
+               [("SL", 0, 8), ("TT", 0, 128), ("dx", 0, 128)], [("X", 0, 2048)])
+        tt(b("Hm"), b("Hf"), b("nh"), MUL)
+        tt(b("T2"), ind(b("As"), b(NLs)), b("hh"), MUL)
+        tt(b("Hf"), b("T2"), b("Hm"), ADD)
+        if not last:
+            cp(b("Hu"), b("Hf"))
+            gather("S", "YG", "Hu", 0, 64)
+        else:
+            dma("Y", T.ycand[:], T.Hf[:], [("Hf", 0, 128)], [])
+        ts(b("Fb"), b(FSs), 32.0, MUL)
+        tt(b("pre"), b("w32"), b("Fb"), MAX)
+
+        tt(b("T1"), ind(b("As"), b(NLr)), b("mm"), MUL)
+        tt(b("Cf"), b("T1"), b("Cm"), ADD)
+        if not last:
+            cp(b("Cu"), b("Cf"))
+        else:
+            dma("Y", T.yctx[:], T.Cf[:], [("Cf", 0, 128)], [])
+
+    for j in range(4):
+        cp(b("W4", 128 * j, 128 * j + 128), b("pre"))
+    for j in range(16):
+        mm(b("PA%d" % (j // 4), j % 4 * 128, j % 4 * 128 + 128), sel("SELT", j), b("pre"))
+    mm(b("PB1", 0, 128), b("BLK"), b(FSs))
+    mm(b("PC", 0, 128), b("NB"), b(FSs), True, False)
+    for i in range(4):
+        tt(b("NQ", 512 * i, 512 * i + 512), b("PA%d" % i), b("W4"), GT)
+        for k in range(4 * i, 4 * i + 4):
+            mm(b("PC", 0, 128), b("ID"), b("NQ", 128 * k, 128 * k + 128), False, k == 15)
+    cp(b("e2"), b("PB1", 0, 128))
+    ts(b("nF2"), b(FSs), -1.0, MUL, 1.0, ADD)
+    ts(b("Fb"), b(FSs), 64.0, MUL)
+    tt(b("DD"), b("PC", 0, 128), b("nF2"), MUL)
+    tt(b("R4"), b("PC", 0, 128), b("Fb"), ADD)
+    tt(b("R2"), b("PC", 0, 128), b("e2"), ADD)
+    tt(b("qq"), b(FSr), b("DD"), MUL)
+    mm(b("PD", 0, 128), b("BLK"), b("qq"))
+    mm(b("PB0", 0, 128), b("BLK"), b(FSr))
+    tt(b("bb"), b("R2"), b("qq"), SUB)
+    tt(b("tq"), b("R4"), b("PD", 0, 128), LT)
+    tt(b("Ro"), b("bb"), b("tq"), ADD)
+    dma("Y", T.ypref[:], T.Ro[:], [("Ro", 0, 128)], [])
+    tt(b("Af"), b("PB0", 0, 128), b("Ai"), ADD)
+    dma("S", T.yfail[:], T.Af[0:128:16, :], [("Af", 0, 128)], [])
+    for sem in sorted(total):
+        if known["Y"].get(sem, 0) < total[sem]:
+            g.sync.wait_ge(T.sem[sem], total[sem])

@@ -16,20 +16,21 @@ for _n, _c, _d in (
         ("NQ", 2048, B16), ("SEL", 2048, B16), ("SELh", 2048, F16), ("SELT", 2048, B16),
         ("ctxi", 128, I32), ("candi", 128, I32), ("prefi", 128, I32), ("fi", 128, I32), ("ff", 128, F32), ("E8", 128, F32),
         ("Rf", 128, F32), ("Cf", 128, F32), ("Hf", 128, F32), ("Cu", 128, U16), ("Hu", 128, U16), ("Ai", 128, I32),
-        ("Am", 128, I32), ("Af", 128, F32), ("W4", 512, B16), ("X4", 512, B16), ("w32", 128, B16), ("pre", 128, B16),
+        ("Am", 128, I32), ("W4", 512, B16), ("X4", 512, B16), ("w32", 128, B16), ("pre", 128, B16),
         ("pci", 8, I32), ("pgi", 8, I32), ("pki", 8, I32), ("pcf", 8, F32), ("pgf", 8, F32), ("pkf", 8, F32), ("nk0", 8, F32),
         ("biask", 8, F32), ("pk16", 8, F32), ("i8", 8, F32), ("i16", 16, F32), ("KJ", 16, F32), ("base", 8, B16),
         ("rowi", 128, F32), ("rowg", 128, F32), ("ID", 128, B16), ("NI", 128, B16), ("BLK", 128, B16), ("HB", 128, B16),
         ("NB", 128, B16), ("B6", 128, B16), ("GM", 128, B16), ("TM", 128, B16), ("JM", 128, B16), ("ACM", 128, B16),
-        ("C512", 128, B16), ("Vb", 128, B16), ("nm", 128, F32), ("mm", 128, F32), ("Cm", 128, F32), ("T1", 128, F32),
-        ("T2", 128, F32), ("nh", 128, F32), ("hh", 128, F32), ("Hm", 128, F32), ("und", 128, B16), ("dsc", 128, B16),
+        ("C512", 128, B16), ("Vb", 128, B16), ("nm", 128, F32), ("mm", 128, F32), ("Cm", 128, F16), ("T1", 128, F16),
+        ("Hh", 128, F16), ("IDh", 128, F16), ("LC", 128, B16), ("LCf", 8, F32), ("IH", 128, B16), ("T2", 128, F16), ("nh", 128, F32), ("hh", 128, F32), ("Hm", 128, F16),
+        ("und", 128, B16), ("dsc", 128, B16),
         ("dx", 128, B16), ("EE", 128, B16), ("OH", 128, B16), ("HOH", 128, F16), ("KOH", 128, B16), ("SL", 8, U16),
         ("UN", 128, B16), ("UW", 128, B16), ("TT", 128, B16), ("NF", 128, B16), ("Fb", 128, B16),
         ("e2", 128, F32), ("nF2", 128, F32), ("DD", 128, F32), ("R4", 128, F32), ("R2", 128, F32), ("qq", 128, B16),
-        ("bb", 128, F32), ("tq", 128, F32), ("Ro", 128, F32)):
+        ("bb", 128, F32), ("tq", 128, F32)):
     SCRATCH[_n] = ("sbuf", [128, _c], _d)
 for _t in range(RO):
-    for _n, _c, _d in (("MW", 256, B16), ("MX", 256, B16), ("NL", 8, U16), ("FS", 128, B16)):
+    for _n, _c, _d in (("MW", 384, B16), ("MX", 128, B16), ("NL", 8, U16), ("FS", 128, B16)):
         SCRATCH["%ss%d" % (_n, _t)] = ("sbuf", [128, _c], _d)
         SCRATCH["%sr%d" % (_n, _t)] = ("sbuf", [128, _c], _d)
 BANKS = ["PA0", "PA1", "PA2", "PA3", "PB0", "PB1", "PC", "PD"]
@@ -134,7 +135,8 @@ def rank_program(g, core, T, topo):
         if bias is None:
             op("S", lambda: g.scalar.activation(out[0], i0[0], f, scale=sc), keys, out[1])
         else:
-            op("S", lambda: g.scalar.activation(out[0], i0[0], f, bias=bias[0], scale=sc), keys + bias[1], out[1])
+            bi, bk = bias if isinstance(bias, tuple) else (bias, [])
+            op("S", lambda: g.scalar.activation(out[0], i0[0], f, bias=bi, scale=sc), keys + bk, out[1])
 
     def mm(out, lt, rh, start=True, stop=True):
         op("P", lambda: g.tensor.matmul(out[0], lt[0], rh[0], start, stop), lt[1] + rh[1], out[1])
@@ -166,10 +168,10 @@ def rank_program(g, core, T, topo):
     def load(q, name, src, p=128):
         dma(q, T[name][0:p, :], src, [], [(name, 0, SCRATCH[name][1][1])])
 
+    load("Y", "ctxi", T.ctx[:])
     load("S", "prefi", T.pref[:])
-    load("S", "ctxi", T.ctx[:])
     load("Y", "X", T.x[:])
-    load("Y", "fi", T.fail0[:], 8)
+    load("S", "fi", T.fail0[:], 8)
     load("Y", "candi", T.cand[:])
     load("Y", "As", T.assoc[:])
 
@@ -177,54 +179,45 @@ def rank_program(g, core, T, topo):
         op("G", lambda: g.iota(out[0], pat, base, cm, allow_small_or_imprecise_dtypes=flag), [], out[1])
 
     iota(b("pci", 0, 1), [[0, 1]], 0, 1, False)
-    iota(b("rowi"), [[1, 128]], 0, 0)
     iota(b("rowg"), [[1, 8], [0, 16]], 0, 0)
+    iota(b("rowi"), [[1, 128]], 0, 0)
     iota(b("i8"), [[256, 8]], 0, 0)
     iota(b("i16"), [[1, 16]], 0, 0)
 
+    fill(b("SEL"), 0.0)
+    fill(b("C512"), 512.0)
     ts(b("pgi", 0, 1), b("pci", 0, 1), 4, SHR)
     ts(b("pki", 0, 1), b("pci", 0, 1), 15, AND)
     cp(b("pcf", 0, 1), b("pci", 0, 1))
     cp(b("pgf", 0, 1), b("pgi", 0, 1))
     cp(b("pkf", 0, 1), b("pki", 0, 1))
-    cp(b("Rf"), b("prefi"))
-    act(b("MWs0", 0, 128), b("Rf"), AF.Exp, scale=-5.0 * LN2)
-    cp(b("Cu"), b("ctxi"))
+    ts(b("BLK"), b("rowg"), col("pgf"), EQ)
+    ts(b("HB"), b("rowg"), col("pgf"), EQ, 0.5, MUL)
     ts(b("ID"), b("rowi"), col("pcf"), EQ)
     ts(b("NI"), b("rowi"), col("pcf"), EQ, -1.0, MUL)
-    ts(b("HB"), b("rowg"), col("pgf"), EQ, 0.5, MUL)
-    ts(b("BLK"), b("rowg"), col("pgf"), EQ)
     tt(b("GM"), b("ID"), b("HB"), SUB)
     ts(b("ACM"), b("NI"), float(2.0 ** 47), MUL)
-    fill(b("C512"), 512.0)
+    ts(b("E8", 0, 128, 1, 8), b("rowg", 0, 128, 1, 8), col("pcf", 0, 8), EQ)
+    cp(b("Cu"), b("ctxi"))
+    cp(b("Rf"), b("prefi"))
+    act(b("MWs0", 0, 128), b("Rf"), AF.Exp, scale=-5.0 * LN2)
+    for gg in range(8):
+        keys = [("SEL", 0, 2048)] if gg == 0 else [("SEL", 2048 + gg, 2049 + gg)]
+        cp((T.SEL[:, 16 * gg:16 * gg + 129 * 15 + 1:129], keys), b("BLK", 16 * gg, 16 * gg + 16))
+    note("SEL", 0, 2048, True, "qV", total["qV"], {"qV": total["qV"]})
     for j in range(4):
         cp(b("W4", 128 * j, 128 * j + 128), b("MWs0", 0, 128))
-    ts(b("E8", 0, 128, 1, 8), b("rowg", 0, 128, 1, 8), col("pcf", 0, 8), EQ)
-    cp(b("ff", 0, 128, 1, 8), b("fi", 0, 128, 1, 8))
-    mm(b("PC", 0, 128), b("E8", 0, 128, 1, 8), b("ff", 0, 128, 1, 8))
-    cp(b("Ai"), b("PC", 0, 128))
-    ts(b("Am"), b("Ai"), 3, AND)
-    ts(b("MWs0", 128, 256), b("Am"), 4, ADD)
+    ts(b("B6"), b("BLK"), 0.0625, MUL)
+    ts(b("nk0", 0, 1), b("pkf", 0, 1), 0.0, NE)
+    ts(b("biask", 0, 1), b("pkf", 0, 1), -LN2, MUL, 120.0 * LN2, ADD)
+    ts(b("pk16", 0, 1), b("pkf", 0, 1), 16.0, MUL)
+    ts(b("KJ"), b("i16"), col("pkf"), EQ)
+    ts(b("base"), b("i8"), col("pk16"), ADD)
+    ts(b("NB"), b("BLK"), -1.0, MUL)
+    tt(b("TM"), b("ID"), b("B6"), SUB)
+    ts(b("JM"), b("GM"), 0.015625, MUL)
+    cp(b("IDh"), b("ID"))
     cp(b("Cf"), b("ctxi"))
-
-    def constants_late():
-        ts(b("B6"), b("BLK"), 0.0625, MUL)
-        tt(b("TM"), b("ID"), b("B6"), SUB)
-        ts(b("NB"), b("BLK"), -1.0, MUL)
-        ts(b("JM"), b("GM"), 0.015625, MUL)
-        ts(b("nk0", 0, 1), b("pkf", 0, 1), 0.0, NE)
-        ts(b("biask", 0, 1), b("pkf", 0, 1), -LN2, MUL, 120.0 * LN2, ADD)
-        ts(b("pk16", 0, 1), b("pkf", 0, 1), 16.0, MUL)
-        ts(b("base"), b("i8"), col("pk16"), ADD)
-        ts(b("KJ"), b("i16"), col("pkf"), EQ)
-        cp(b("Hu"), b("candi"))
-        cp(b("Hf"), b("candi"))
-
-    def selectors():
-        fill(b("SEL"), 0.0)
-        for gg in range(8):
-            cp((T.SEL[:, 16 * gg:16 * gg + 129 * 15 + 1:129], [("SEL", 0, 2048)]), b("BLK", 16 * gg, 16 * gg + 16))
-        cp(b("SELh"), b("SEL"))
 
     def gather(q, dst, offs, s0, s1):
         out = b(dst, 16 * s0, 16 * s1)
@@ -238,28 +231,35 @@ def rank_program(g, core, T, topo):
         q_rank, s_rank = (rank + STEP[t]) % n_ranks, (rank - STEP[t]) % n_ranks
         MWs, MWr, MXs, MXr = "MWs%d" % t, "MWr%d" % t, "MXs%d" % t, "MXr%d" % t
         NLs, NLr, FSs, FSr = "NLs%d" % t, "NLr%d" % t, "FSs%d" % t, "FSr%d" % t
+        FSo = "FSr%d" % (t - 1)
         last = t == RO - 1
 
         gather("V", "XG", "Cu", 0, 32)
         gather("S", "XG", "Cu", 32, 64)
         gather("V", "XG", "Cu", 64, 96)
         gather("S", "XG", "Cu", 96, 128)
+        if t:
+            tt(b("T2"), ind(b("As"), b("NLs%d" % (t - 1))), b("hh"), MUL)
+            mm(b("PD", 128, 256), b("IDh"), b("Hm"), True, False)
         for h in range(2):
             for k in range(1, 16):
                 o = b("PA%d" % ((k - 1) // 4), (k - 1) % 4 * 128 + 64 * h, (k - 1) % 4 * 128 + 64 * h + 64)
                 mm(o, b("ID"), b("XG", 1024 * h + k, 1024 * h + 1024, 16), True, False)
                 mm(o, b("NI"), b("XG", 1024 * h, 1024 * h + 1024, 16), False, True)
+        act(b(MWs, 256, 384), b("XG", 0, 2048, 16), AF.Copy)
         if t:
-            tt(b(MWs, 0, 128), b("pre"), b("FSr%d" % (t - 1)), MAX)
+            mm(b("PD", 128, 256), b("IDh"), b("T2"), False, True)
+            tt(b(MWs, 0, 128), b("pre"), b(FSo), MAX)
             for j in range(4):
                 cp(b("W4", 128 * j, 128 * j + 128), b(MWs, 0, 128))
-        cp(b(MXs, 128, 256), b("XG", 0, 2048, 16))
-        if t:
-            mm(b("PC", 0, 128), b("BLK"), b("FSr%d" % (t - 1)))
-            tt(b("Ai"), b("PC", 0, 128), b("Ai"), ADD)
+            cp(b("Hu"), b("PD", 128, 256))
+        else:
+            cp(b("ff", 0, 128, 1, 8), b("fi", 0, 128, 1, 8))
+            mm(b("PC", 0, 128), b("E8", 0, 128, 1, 8), b("ff", 0, 128, 1, 8))
+            cp(b("Ai"), b("PC", 0, 128))
             ts(b("Am"), b("Ai"), 3, AND)
             ts(b(MWs, 128, 256), b("Am"), 4, ADD)
-        send("MW", t, q_rank, s_rank)
+            send("MW", t, q_rank, s_rank)
         width = (512, 512, 512, 384)
         dbank = ("PB0", "PB1", "PA0", "PA1")
         for i in range(4):
@@ -278,64 +278,84 @@ def rank_program(g, core, T, topo):
         mm(b("PC", 0, 128), b("ID"), b("C512"), True, False)
         for k in range(15):
             mm(b("PC", 0, 128), b("ACM"), b("RL", 128 * k, 128 * k + 128), False, k == 14)
-        tt(b(MXs, 0, 128), b("PC", 0, 128), b(MXs, 128, 256), MAX)
+        tt(b(MXs), b("PC", 0, 128), b(MWs, 256, 384), MAX)
         send("MX", t, q_rank, s_rank)
 
-        if t == 0:
-            constants_late()
-            gather("S", "YG", "Hu", 0, 64)
-        gather("S", "YG", "Hu", 96, 128)
-        gather("V", "YG", "Hu", 64, 96)
-        if t == 0:
-            selectors()
-        for k in range(16):
-            mm(b("PA%d" % (k // 4), k % 4 * 128, k % 4 * 128 + 128), b("ID"), b("YG", k, 2048, 16))
+        if t:
+            mm(b("PB0", 0, 128), b("BLK"), b(FSo))
+            tt(b("Ai"), b("PB0", 0, 128), b("Ai"), ADD)
+            act(b("Cf"), b("PD", 0, 128), AF.Copy)
+            act(b("Hf"), b("PD", 128, 256), AF.Copy)
+            ts(b("Am"), b("Ai"), 3, AND)
+            ts(b(MWs, 128, 256), b("Am"), 4, ADD)
+            send("MW", t, q_rank, s_rank)
+        else:
+            cp(b("Hu"), b("candi"))
+            cp(b("Hf"), b("candi"))
+        gather("S", "YG", "Hu", 0, 96)
+        gather("V", "YG", "Hu", 96, 128)
         for k in range(1, 16):
             mm(b("PD", 0, 128), sel("SEL", k), b("Z", 128 * (k - 1), 128 * k), k == 1, k == 15)
         cp(b("Vb"), b("PD", 0, 128))
         mm(b("PB0", 0, 128), b("TM"), b("Vb"))
-        ts(b("w32"), b(MWs, 0, 128), float(2.0 ** -10), MUL)
+        cp(b("Hh"), b("Hf"))
         ts(b("nm"), b("PB0", 0, 128), 0.0, LE, col("nk0"), MUL)
-        ts(b("mm"), b("nm"), -1.0, MUL, 1.0, ADD)
+        for k in range(12):
+            mm(b("PA%d" % (k // 4), k % 4 * 128, k % 4 * 128 + 128), b("ID"), b("YG", k, 2048, 16))
         tt(b("Cm"), b("Cf"), b("nm"), MUL)
-        if t < 3:
-            for j in range(6 * t, min(16, 6 * t + 6)):
-                act(sel("SELT", j), b("BLK"), AF.Copy, scale=col("KJ", j))
+        if t == 0:
+            cp(b("SELh"), b("SEL"))
+            ts(b("LCf", 0, 1), b("pkf", 0, 1), 7.5, GT, -0.5 / 512, MUL)
+            ts(b("LCf", 1, 2), b("LCf", 0, 1), 4.0 / 512, ADD)
+            ts(b("LC"), b("ID"), col("LCf", 1), MUL)
+            ts(b("IH"), b("ID"), 0.5, MUL)
+        act(b("mm"), b("nm"), AF.Identity, scale=-1.0, bias=1.0)
+        act(b("w32"), b(MWs, 0, 128), AF.Copy, scale=float(2.0 ** -10))
 
         for j in range(4):
-            act(b("X4", 128 * j, 128 * j + 128), b(MXr, 0, 128), AF.Copy)
+            act(b("X4", 128 * j, 128 * j + 128), b(MXr), AF.Copy)
         for k in range(4):
-            tt(b("NQ", 128 * k, 128 * k + 128), b("PA0", 128 * k, 128 * k + 128), b(MXr, 0, 128), NE)
-        ts(b("und"), b(MXr, 0, 128), 512.0, EQ)
+            tt(b("NQ", 128 * k, 128 * k + 128), b("PA0", 128 * k, 128 * k + 128), b(MXr), NE)
+        ts(b("und"), b(MXr), 512.0, EQ)
+        for k in range(12, 16):
+            o = b("PA3", k % 4 * 128, k % 4 * 128 + 128)
+            mm(o, b("ID"), b("YG", k, 2048, 16), True, False)
+            mm(o, b("NI"), b(MXr), False, True)
+        act(b("PA3"), b("PA3"), AF.Sign)
+        act(b("NQ", 1536, 2048), b("PA3"), AF.Square)
+        tt(b("NQ", 512, 1024), b("PA1"), b("X4"), NE)
+        for i in range(2):
+            tt(b("NQ", 1024 + 256 * i, 1280 + 256 * i), b("PA2", 256 * i, 256 * i + 256), b("X4", 256 * i, 256 * i + 256), NE)
         mm(b("PC", 0, 128), b("NB"), b("und"), True, False)
-        for i in range(1, 4):
-            tt(b("NQ", 512 * i, 512 * i + 512), b("PA%d" % i), b("X4"), NE)
         for k in range(16):
             mm(b("PC", 0, 128), sel("SEL", k), b("NQ", 128 * k, 128 * k + 128), False, k == 15)
         act(b("EE"), b("PC", 0, 128), AF.Exp, scale=-16.0 * LN2, bias=col("biask"))
         mm(b("PD", 0, 128), b("HB"), b("EE"))
+        mm(b("PA2", 0, 128), b("IDh"), b("Hh"))
         if not last:
-            ts(b("dsc"), b(MXr, 0, 128), 512.0, NE)
-            tt(b("dx"), b(MXr, 128, 256), b("dsc"), MUL)
+            ts(b("dsc"), b(MXr), 512.0, NE)
         tt(b("OH"), b("EE"), b("PD", 0, 128), GT)
-        tt(b("HOH"), b("OH"), b("Hf"), MUL)
+        tt(b("HOH"), b("PA2", 0, 128), b("OH"), MUL)
         for a in range(16):
             mm(b("PB0", 0, 8), sel("SELh", a), b("HOH", a, 128, 16), a == 0, a == 15)
+        mm(b("PA3", 0, 128), b("ID"), b(MWr, 0, 128))
         if not last:
             act(b("KOH"), b("OH"), AF.Copy, scale=col("pkf"))
             mm(b("PB1", 0, 8), b("ID"), b("base"), True, False)
-            for a in range(16):
-                mm(b("PB1", 0, 8), sel("SEL", a), b("KOH", a, 128, 16), False, a == 15)
-        ts(b("nh"), b("PC", 0, 128), 0.0, LE)
-        ts(b("hh"), b("PC", 0, 128), 0.0, GT)
+        act(b("nh"), b("PC", 0, 128), AF.Relu, scale=-1.0, bias=1.0)
+        act(b("hh"), b("PC", 0, 128), AF.Sign)
+        if not last:
+            tt(b("dx"), b(MWr, 256, 384), b("dsc"), MUL)
         cp(b(NLs), b("PB0", 0, 8))
         send("NL", t, s_rank, q_rank)
 
-        tt(b("UN"), ind(b("X"), b(NLs)), b(MXr, 128, 256), NE)
+        tt(b("UN"), ind(b("X"), b(NLs)), b(MWr, 256, 384), NE)
         mm(b("PA0", 0, 128), b("BLK"), b("UN"))
-        tt(b("UW"), b("UN"), b(MWr, 0, 128), MUL)
+        tt(b("UW"), b("PA3", 0, 128), b("UN"), MUL)
         mm(b("PA1", 0, 128), b("JM"), b("UW"))
         if not last:
+            for a in range(16):
+                mm(b("PB1", 0, 8), sel("SEL", a), b("KOH", a, 128, 16), False, a == 15)
             tt(b("TT"), ind(b("X"), b(NLs)), b("und"), MUL)
         tt(b("NF"), b("PA0", 0, 128), b(MWr, 128, 256), LE)
         tt(b(FSs), b("PA1", 0, 128), b("NF"), GT)
@@ -345,49 +365,58 @@ def rank_program(g, core, T, topo):
             win = ind(b("X"), b("SL"))
             op("V", lambda: g.vector.tensor_tensor(win[0], T.TT[:], T.dx[:], ADD),
                [("SL", 0, 8), ("TT", 0, 128), ("dx", 0, 128)], [("X", 0, 2048)])
+        act(b("Fb"), b(FSs), AF.Copy, scale=32.0)
+        mm(b("PD", 0, 128), b("IDh"), b("Cm"), True, False)
         tt(b("Hm"), b("Hf"), b("nh"), MUL)
-        tt(b("T2"), ind(b("As"), b(NLs)), b("hh"), MUL)
-        tt(b("Hf"), b("T2"), b("Hm"), ADD)
-        if not last:
-            cp(b("Hu"), b("Hf"))
-            gather("S", "YG", "Hu", 0, 64)
-        else:
+        if last:
+            tt(b("T2"), ind(b("As"), b(NLs)), b("hh"), MUL)
+            tt(b("Hf"), b("T2"), b("Hm"), ADD)
             dma("Y", T.ycand[:], T.Hf[:], [("Hf", 0, 128)], [])
-        ts(b("Fb"), b(FSs), 32.0, MUL)
         tt(b("pre"), b("w32"), b("Fb"), MAX)
+        if last:
+            break
 
         tt(b("T1"), ind(b("As"), b(NLr)), b("mm"), MUL)
-        tt(b("Cf"), b("T1"), b("Cm"), ADD)
-        if not last:
-            cp(b("Cu"), b("Cf"))
-        else:
-            dma("Y", T.yctx[:], T.Cf[:], [("Cf", 0, 128)], [])
+        mm(b("PD", 0, 128), b("IDh"), b("T1"), False, True)
+        cp(b("Cu"), b("PD", 0, 128))
+        for j in range(6 * t, min(16, 6 * t + 6)):
+            act(sel("SELT", j), b("BLK"), AF.Copy, scale=col("KJ", j))
 
+    for j in range(8):
+        o = b("PA%d" % (2 + j // 4), j % 4 * 128, j % 4 * 128 + 128)
+        mm(o, sel("SELT", 8 + j), b("pre"), True, False)
+        mm(o, b("NI"), b("pre"), False, True)
+        mm(b("PA%d" % (j // 4), j % 4 * 128, j % 4 * 128 + 128), sel("SELT", j), b("pre"))
     for j in range(4):
         cp(b("W4", 128 * j, 128 * j + 128), b("pre"))
-    for j in range(16):
-        mm(b("PA%d" % (j // 4), j % 4 * 128, j % 4 * 128 + 128), sel("SELT", j), b("pre"))
     mm(b("PB1", 0, 128), b("BLK"), b(FSs))
     mm(b("PC", 0, 128), b("NB"), b(FSs), True, False)
-    for i in range(4):
+    mm(b("PC", 0, 128), b("LC"), b("C512"), False, False)
+    for i in range(2):
+        act(b("NQ", 1024 + 512 * i, 1536 + 512 * i), b("PA%d" % (2 + i)), AF.Sign)
         tt(b("NQ", 512 * i, 512 * i + 512), b("PA%d" % i), b("W4"), GT)
         for k in range(4 * i, 4 * i + 4):
-            mm(b("PC", 0, 128), b("ID"), b("NQ", 128 * k, 128 * k + 128), False, k == 15)
-    cp(b("e2"), b("PB1", 0, 128))
-    ts(b("nF2"), b(FSs), -1.0, MUL, 1.0, ADD)
-    ts(b("Fb"), b(FSs), 64.0, MUL)
+            mm(b("PC", 0, 128), b("ID"), b("NQ", 128 * k, 128 * k + 128), False, False)
+            mm(b("PC", 0, 128), b("IH"), b("NQ", 1024 + 128 * k, 1152 + 128 * k), False, k == 7)
+    act(b("e2"), b("PB1", 0, 128), AF.Copy)
+    act(b("nF2"), b(FSs), AF.Identity, scale=-1.0, bias=1.0)
+    act(b("Fb"), b(FSs), AF.Copy, scale=64.0)
+    tt(b("T1"), ind(b("As"), b(NLr)), b("mm"), MUL)
+    mm(b("PD", 0, 128), b("IDh"), b("T1"), False, True)
+    act(b("Cf"), b("PD", 0, 128), AF.Copy)
+    dma("Y", T.yctx[:], T.Cf[:], [("Cf", 0, 128)], [])
     tt(b("DD"), b("PC", 0, 128), b("nF2"), MUL)
+    tt(b("qq"), b(FSr), b("DD"), MUL)
+    mm(b("PB1", 0, 128), b("BLK"), b("qq"))
+    mm(b("PB0", 0, 128), b("BLK"), b(FSr))
     tt(b("R4"), b("PC", 0, 128), b("Fb"), ADD)
     tt(b("R2"), b("PC", 0, 128), b("e2"), ADD)
-    tt(b("qq"), b(FSr), b("DD"), MUL)
-    mm(b("PD", 0, 128), b("BLK"), b("qq"))
-    mm(b("PB0", 0, 128), b("BLK"), b(FSr))
     tt(b("bb"), b("R2"), b("qq"), SUB)
-    tt(b("tq"), b("R4"), b("PD", 0, 128), LT)
-    tt(b("Ro"), b("bb"), b("tq"), ADD)
-    dma("Y", T.ypref[:], T.Ro[:], [("Ro", 0, 128)], [])
-    tt(b("Af"), b("PB0", 0, 128), b("Ai"), ADD)
-    dma("S", T.yfail[:], T.Af[0:128:16, :], [("Af", 0, 128)], [])
+    tt(b("tq"), b("R4"), b("PB1", 0, 128), LT)
+    tt(b("bb"), b("bb"), b("tq"), ADD)
+    dma("Y", T.ypref[:], T.bb[:], [("bb", 0, 128)], [])
+    tt(b("Rf"), b("PB0", 0, 128), b("Ai"), ADD)
+    dma("S", T.yfail[:], T.Rf[0:128:16, :], [("Rf", 0, 128)], [])
     for sem in sorted(total):
         if known["Y"].get(sem, 0) < total[sem]:
             g.sync.wait_ge(T.sem[sem], total[sem])

import math
from concourse.mybir import AluOpType, ActivationFunctionType

ADD, SUB, MUL, MAX, MIN = AluOpType.add, AluOpType.subtract, AluOpType.mult, AluOpType.max, AluOpType.min
GT, LT, LE, EQ, NE = AluOpType.is_gt, AluOpType.is_lt, AluOpType.is_le, AluOpType.is_equal, AluOpType.not_equal
SHR, AND = AluOpType.logical_shift_right, AluOpType.bitwise_and
AF = ActivationFunctionType
LN2 = math.log(2.0)
STEP = (4, 1, 3, 6)
RO = 4
B16, F32, I32, U16, F16 = "bfloat16", "float32", "int32", "uint16", "float16"

SCRATCH = {}
for _n, _c, _d in (
        ("X", 2048, B16), ("As", 2048, I32), ("XG", 2048, B16), ("YG", 2048, B16), ("Z", 2048, B16), ("RL", 2048, B16),
        ("NQ", 2048, B16), ("SEL", 2048, B16), ("SELh", 2048, F16), ("SELT", 2048, B16),
        ("ctxi", 128, I32), ("candi", 128, I32), ("prefi", 128, I32), ("fi", 128, I32), ("ff", 128, F32), ("E8", 128, F32),
        ("Rf", 128, F32), ("Cf", 128, F32), ("Hf", 128, F32), ("Cu", 128, U16), ("Hu", 128, U16), ("Ai", 128, I32),
        ("Am", 128, I32), ("W4", 512, B16), ("X4", 512, B16), ("w32", 128, B16), ("pre", 128, B16),
        ("pci", 8, I32), ("pgi", 8, I32), ("pki", 8, I32), ("pcf", 8, F32), ("pgf", 8, F32), ("pkf", 8, F32), ("nk0", 8, F32),
        ("biask", 8, F32), ("pk16", 8, F32), ("i8", 8, F32), ("i16", 16, F32), ("KJ", 16, F32), ("base", 8, B16),
        ("rowi", 128, F32), ("rowg", 128, F32), ("ID", 128, B16), ("NI", 128, B16), ("BLK", 128, B16), ("HB", 128, B16),
        ("NB", 128, B16), ("B6", 128, B16), ("GM", 128, B16), ("TM", 128, B16), ("JM", 128, B16), ("ACM", 128, B16),
        ("C512", 128, B16), ("Vb", 128, B16), ("nm", 128, F32), ("mm", 128, F32), ("Cm", 128, F16), ("T1", 128, F16),
        ("Hh", 128, F16), ("IDh", 128, F16), ("LC", 128, B16), ("LCf", 8, F32), ("IH", 128, B16), ("T2", 128, F16), ("nh", 128, F32), ("hh", 128, F32), ("Hm", 128, F16),
        ("und", 128, B16), ("dsc", 128, B16),
        ("dx", 128, B16), ("EE", 128, B16), ("OH", 128, B16), ("HOH", 128, F16), ("KOH", 128, B16), ("SL", 8, U16),
        ("UN", 128, B16), ("UW", 128, B16), ("TT", 128, B16), ("NF", 128, B16), ("Fb", 128, B16),
        ("e2", 128, F32), ("nF2", 128, F32), ("DD", 128, F32), ("R4", 128, F32), ("R2", 128, F32), ("qq", 128, B16),
        ("bb", 128, F32), ("tq", 128, F32)):
    SCRATCH[_n] = ("sbuf", [128, _c], _d)
for _t in range(RO):
    for _n, _c, _d in (("MW", 384, B16), ("MX", 128, B16), ("NL", 8, U16), ("FS", 128, B16)):
        SCRATCH["%ss%d" % (_n, _t)] = ("sbuf", [128, _c], _d)
        SCRATCH["%sr%d" % (_n, _t)] = ("sbuf", [128, _c], _d)
BANKS = ["PA0", "PA1", "PA2", "PA3", "PB0", "PB1", "PC", "PD"]
for _n in BANKS:
    SCRATCH[_n] = ("psum", [128, 512], "float32")
KINDS = ["MW", "MX", "NL", "FS"]
SEMAPHORES = ["qV", "qS", "qP", "qG", "sent"] + ["d%d" % _i for _i in range(12)] + \
             ["a%s%d" % (_k, _t) for _k in KINDS for _t in range(RO)]


def rank_program(g, core, T, topo):
    rank = T.rank_of(core)
    if rank is None:
        return
    n_ranks = len(T.cores)
    queue = {"V": g.vector, "S": g.scalar, "P": g.tensor, "G": g, "Y": g.sync}
    known = {q: {} for q in queue}
    total = {}
    acc = {}
    count = [0, 0]

    def need(q, recs):
        for idx, sem, val, clock in sorted(recs, key=lambda r: -r[0]):
            if known[q].get(sem, 0) >= val:
                continue
            queue[q].wait_ge(T.sem[sem], val)
            for s, v in clock.items():
                if known[q].get(s, 0) < v:
                    known[q][s] = v

    def note(name, c0, c1, write, sem, val, clock):
        acc.setdefault(name, {})[(sem, c0, c1, write)] = (count[0], val, clock)

    def op(q, call, reads, writes, sem=None, inc=1):
        own = "q" + q
        recs = []
        for keys, w in ((reads, False), (writes, True)):
            for name, c0, c1 in keys:
                bank = name in BANKS
                for (s, a, b, wr), (idx, val, clock) in acc.get(name, {}).items():
                    if not bank and (b <= c0 or c1 <= a):
                        continue
                    if s == own:
                        if (w and q == "P") or not wr or (bank and (b <= c0 or c1 <= a)):
                            continue
                    elif not bank and not w and not wr:
                        continue
                    recs.append((idx, s, val, clock))
        need(q, recs)
        sem = sem or own
        total[sem] = total.get(sem, 0) + inc
        call().then_inc(T.sem[sem], inc)
        count[0] += 1
        clock = dict(known[q])
        clock[sem] = total[sem]
        for name, c0, c1 in reads:
            note(name, c0, c1, False, sem, total[sem], clock)
        for name, c0, c1 in writes:
            note(name, c0, c1, True, sem, total[sem], clock)

    def b(name, c0=0, c1=None, st=1, p=128):
        if c1 is None:
            c1 = SCRATCH[name][1][1] if c0 == 0 else c0 + 128
        ap = T[name][0:p, c0:c1] if st == 1 else T[name][0:p, c0:c1:st]
        return ap, [(name, c0, c1)]

    def col(name, j=0, p=128):
        return T[name][0:p, j:j + 1], [(name, j, j + 1)]

    def ind(win, offs):
        return win[0].indirect(offs[0]), win[1] + offs[1]

    def tt(out, i0, i1, o):
        op("V", lambda: g.vector.tensor_tensor(out[0], i0[0], i1[0], o), i0[1] + i1[1], out[1])

    def ts(out, i0, s1, o0, s2=None, o1=None):
        keys = list(i0[1])
        v = []
        for s in (s1, s2):
            if isinstance(s, tuple):
                keys += s[1]
                v.append(s[0])
            else:
                v.append(s)
        if o1 is None:
            op("V", lambda: g.vector.tensor_scalar(out[0], i0[0], v[0], None, o0), keys, out[1])
        else:
            op("V", lambda: g.vector.tensor_scalar(out[0], i0[0], v[0], v[1], o0, o1), keys, out[1])

    def cp(out, i0):
        op("V", lambda: g.vector.tensor_copy(out[0], i0[0]), i0[1], out[1])

    def fill(out, v):
        op("V", lambda: g.vector.memset(out[0], v), [], out[1])

    def act(out, i0, f, scale=1.0, bias=None):
        keys = list(i0[1])
        sc = scale
        if isinstance(scale, tuple):
            keys += scale[1]
            sc = scale[0]
        if bias is None:
            op("S", lambda: g.scalar.activation(out[0], i0[0], f, scale=sc), keys, out[1])
        else:
            bi, bk = bias if isinstance(bias, tuple) else (bias, [])
            op("S", lambda: g.scalar.activation(out[0], i0[0], f, bias=bi, scale=sc), keys + bk, out[1])

    def mm(out, lt, rh, start=True, stop=True):
        op("P", lambda: g.tensor.matmul(out[0], lt[0], rh[0], start, stop), lt[1] + rh[1], out[1])

    def dma(q, out, i0, reads, writes):
        s = "d%d" % count[1]
        count[1] += 1
        op(q, lambda: queue[q].dma_start(out, i0), reads, writes, s, 16)

    def send(kind, t, dst_rank, src_rank):
        dst = T.cores[dst_rank]
        s, r, name = "%ss%d" % (kind, t), "%sr%d" % (kind, t), "a%s%d" % (kind, t)
        recs = [(i, sm, v, c) for (sm, a, e, wr), (i, v, c) in acc.get(s, {}).items() if wr]
        need("G", recs)
        rid, pid = topo.addr(dst, core)
        ne = len(topo.engines(core, dst))
        g.remote_dma(out_ap=T[r][:], in_ap=T[s][:], remote_sem=T.sem[name], local_sem=T.sem["sent"], pid=pid, routing_id=rid,
                     dma_engine_mask=topo.mask(core, dst))
        total["sent"] = total.get("sent", 0) + ne
        src = T.cores[src_rank]
        arrive = len(topo.engines(src, core))
        total[name] = arrive
        count[0] += 1
        note(r, 0, SCRATCH[r][1][1], True, name, arrive, {name: arrive})

    def sel(name, k):
        return b(name, 128 * k, 128 * k + 128)

    def load(q, name, src, p=128):
        dma(q, T[name][0:p, :], src, [], [(name, 0, SCRATCH[name][1][1])])

    load("Y", "ctxi", T.ctx[:])
    load("S", "prefi", T.pref[:])
    load("Y", "X", T.x[:])
    load("S", "fi", T.fail0[:], 8)
    load("Y", "candi", T.cand[:])
    load("Y", "As", T.assoc[:])

    def iota(out, pat, base, cm, flag=True):
        op("G", lambda: g.iota(out[0], pat, base, cm, allow_small_or_imprecise_dtypes=flag), [], out[1])

    iota(b("pci", 0, 1), [[0, 1]], 0, 1, False)
    iota(b("rowg"), [[1, 8], [0, 16]], 0, 0)
    iota(b("rowi"), [[1, 128]], 0, 0)
    iota(b("i8"), [[256, 8]], 0, 0)
    iota(b("i16"), [[1, 16]], 0, 0)

    fill(b("SEL"), 0.0)
    fill(b("C512"), 512.0)
    ts(b("pgi", 0, 1), b("pci", 0, 1), 4, SHR)
    ts(b("pki", 0, 1), b("pci", 0, 1), 15, AND)
    cp(b("pcf", 0, 1), b("pci", 0, 1))
    cp(b("pgf", 0, 1), b("pgi", 0, 1))
    cp(b("pkf", 0, 1), b("pki", 0, 1))
    ts(b("BLK"), b("rowg"), col("pgf"), EQ)
    ts(b("HB"), b("rowg"), col("pgf"), EQ, 0.5, MUL)
    ts(b("ID"), b("rowi"), col("pcf"), EQ)
    ts(b("NI"), b("rowi"), col("pcf"), EQ, -1.0, MUL)
    tt(b("GM"), b("ID"), b("HB"), SUB)
    ts(b("ACM"), b("NI"), float(2.0 ** 47), MUL)
    ts(b("E8", 0, 128, 1, 8), b("rowg", 0, 128, 1, 8), col("pcf", 0, 8), EQ)
    cp(b("Cu"), b("ctxi"))
    cp(b("Rf"), b("prefi"))
    act(b("MWs0", 0, 128), b("Rf"), AF.Exp, scale=-5.0 * LN2)
    for gg in range(8):
        keys = [("SEL", 0, 2048)] if gg == 0 else [("SEL", 2048 + gg, 2049 + gg)]
        cp((T.SEL[:, 16 * gg:16 * gg + 129 * 15 + 1:129], keys), b("BLK", 16 * gg, 16 * gg + 16))
    note("SEL", 0, 2048, True, "qV", total["qV"], {"qV": total["qV"]})
    for j in range(4):
        cp(b("W4", 128 * j, 128 * j + 128), b("MWs0", 0, 128))
    ts(b("B6"), b("BLK"), 0.0625, MUL)
    ts(b("nk0", 0, 1), b("pkf", 0, 1), 0.0, NE)
    ts(b("biask", 0, 1), b("pkf", 0, 1), -LN2, MUL, 120.0 * LN2, ADD)
    ts(b("pk16", 0, 1), b("pkf", 0, 1), 16.0, MUL)
    ts(b("KJ"), b("i16"), col("pkf"), EQ)
    ts(b("base"), b("i8"), col("pk16"), ADD)
    ts(b("NB"), b("BLK"), -1.0, MUL)
    tt(b("TM"), b("ID"), b("B6"), SUB)
    ts(b("JM"), b("GM"), 0.015625, MUL)
    cp(b("IDh"), b("ID"))
    cp(b("Cf"), b("ctxi"))

    def gather(q, dst, offs, s0, s1):
        out = b(dst, 16 * s0, 16 * s1)
        src = ind(b("X"), b(offs, s0, s1))
        if q == "V":
            cp(out, src)
        else:
            act(out, src, AF.Copy)

    for t in range(RO):
        q_rank, s_rank = (rank + STEP[t]) % n_ranks, (rank - STEP[t]) % n_ranks
        MWs, MWr, MXs, MXr = "MWs%d" % t, "MWr%d" % t, "MXs%d" % t, "MXr%d" % t
        NLs, NLr, FSs, FSr = "NLs%d" % t, "NLr%d" % t, "FSs%d" % t, "FSr%d" % t
        FSo = "FSr%d" % (t - 1)
        last = t == RO - 1

        gather("V", "XG", "Cu", 0, 32)
        gather("S", "XG", "Cu", 32, 64)
        gather("V", "XG", "Cu", 64, 96)
        gather("S", "XG", "Cu", 96, 128)
        if t:
            tt(b("T2"), ind(b("As"), b("NLs%d" % (t - 1))), b("hh"), MUL)
            mm(b("PD", 128, 256), b("IDh"), b("Hm"), True, False)
        for h in range(2):
            for k in range(1, 16):
                o = b("PA%d" % ((k - 1) // 4), (k - 1) % 4 * 128 + 64 * h, (k - 1) % 4 * 128 + 64 * h + 64)
                mm(o, b("ID"), b("XG", 1024 * h + k, 1024 * h + 1024, 16), True, False)
                mm(o, b("NI"), b("XG", 1024 * h, 1024 * h + 1024, 16), False, True)
        act(b(MWs, 256, 384), b("XG", 0, 2048, 16), AF.Copy)
        if t:
            mm(b("PD", 128, 256), b("IDh"), b("T2"), False, True)
            tt(b(MWs, 0, 128), b("pre"), b(FSo), MAX)
            for j in range(4):
                cp(b("W4", 128 * j, 128 * j + 128), b(MWs, 0, 128))
            cp(b("Hu"), b("PD", 128, 256))
        else:
            cp(b("ff", 0, 128, 1, 8), b("fi", 0, 128, 1, 8))
            mm(b("PC", 0, 128), b("E8", 0, 128, 1, 8), b("ff", 0, 128, 1, 8))
            cp(b("Ai"), b("PC", 0, 128))
            ts(b("Am"), b("Ai"), 3, AND)
            ts(b(MWs, 128, 256), b("Am"), 4, ADD)
            send("MW", t, q_rank, s_rank)
        width = (512, 512, 512, 384)
        dbank = ("PB0", "PB1", "PA0", "PA1")
        for i in range(4):
            n = width[i]
            act(b("PA%d" % i, 0, n), b("PA%d" % i, 0, n), AF.Abs, scale=64.0)
        for i in range(4):
            n = width[i]
            tt(b("Z", 512 * i, 512 * i + n), b("PA%d" % i, 0, n), b("W4", 0, n), MIN)
            mm(b(dbank[i], 0, n), b("GM"), b("Z", 512 * i, 512 * i + n))
        for i in range(4):
            n = width[i]
            if i < 2:
                act(b("RL", 512 * i, 512 * i + n), b(dbank[i], 0, n), AF.Relu, scale=float(2.0 ** 70))
            else:
                ts(b("RL", 512 * i, 512 * i + n), b(dbank[i], 0, n), 0.0, MAX, float(2.0 ** 70), MUL)
        mm(b("PC", 0, 128), b("ID"), b("C512"), True, False)
        for k in range(15):
            mm(b("PC", 0, 128), b("ACM"), b("RL", 128 * k, 128 * k + 128), False, k == 14)
        tt(b(MXs), b("PC", 0, 128), b(MWs, 256, 384), MAX)
        send("MX", t, q_rank, s_rank)

        if t:
            mm(b("PB0", 0, 128), b("BLK"), b(FSo))
            tt(b("Ai"), b("PB0", 0, 128), b("Ai"), ADD)
            act(b("Cf"), b("PD", 0, 128), AF.Copy)
            act(b("Hf"), b("PD", 128, 256), AF.Copy)
            ts(b("Am"), b("Ai"), 3, AND)
            ts(b(MWs, 128, 256), b("Am"), 4, ADD)
            send("MW", t, q_rank, s_rank)
        else:
            cp(b("Hu"), b("candi"))
            cp(b("Hf"), b("candi"))
        gather("S", "YG", "Hu", 0, 96)
        gather("V", "YG", "Hu", 96, 128)
        for k in range(1, 16):
            mm(b("PD", 0, 128), sel("SEL", k), b("Z", 128 * (k - 1), 128 * k), k == 1, k == 15)
        cp(b("Vb"), b("PD", 0, 128))
        mm(b("PB0", 0, 128), b("TM"), b("Vb"))
        cp(b("Hh"), b("Hf"))
        ts(b("nm"), b("PB0", 0, 128), 0.0, LE, col("nk0"), MUL)
        for k in range(12):
            mm(b("PA%d" % (k // 4), k % 4 * 128, k % 4 * 128 + 128), b("ID"), b("YG", k, 2048, 16))
        tt(b("Cm"), b("Cf"), b("nm"), MUL)
        if t == 0:
            cp(b("SELh"), b("SEL"))
            ts(b("LCf", 0, 1), b("pkf", 0, 1), 7.5, GT, -0.5 / 512, MUL)
            ts(b("LCf", 1, 2), b("LCf", 0, 1), 4.0 / 512, ADD)
            ts(b("LC"), b("ID"), col("LCf", 1), MUL)
            ts(b("IH"), b("ID"), 0.5, MUL)
        act(b("mm"), b("nm"), AF.Identity, scale=-1.0, bias=1.0)
        act(b("w32"), b(MWs, 0, 128), AF.Copy, scale=float(2.0 ** -10))

        for j in range(4):
            act(b("X4", 128 * j, 128 * j + 128), b(MXr), AF.Copy)
        for k in range(4):
            tt(b("NQ", 128 * k, 128 * k + 128), b("PA0", 128 * k, 128 * k + 128), b(MXr), NE)
        ts(b("und"), b(MXr), 512.0, EQ)
        for k in range(12, 16):
            o = b("PA3", k % 4 * 128, k % 4 * 128 + 128)
            mm(o, b("ID"), b("YG", k, 2048, 16), True, False)
            mm(o, b("NI"), b(MXr), False, True)
        act(b("PA3"), b("PA3"), AF.Sign)
        act(b("NQ", 1536, 2048), b("PA3"), AF.Square)
        tt(b("NQ", 512, 1024), b("PA1"), b("X4"), NE)
        for i in range(2):
            tt(b("NQ", 1024 + 256 * i, 1280 + 256 * i), b("PA2", 256 * i, 256 * i + 256), b("X4", 256 * i, 256 * i + 256), NE)
        mm(b("PC", 0, 128), b("NB"), b("und"), True, False)
        for k in range(16):
            mm(b("PC", 0, 128), sel("SEL", k), b("NQ", 128 * k, 128 * k + 128), False, k == 15)
        act(b("EE"), b("PC", 0, 128), AF.Exp, scale=-16.0 * LN2, bias=col("biask"))
        mm(b("PD", 0, 128), b("HB"), b("EE"))
        mm(b("PA2", 0, 128), b("IDh"), b("Hh"))
        if not last:
            ts(b("dsc"), b(MXr), 512.0, NE)
        tt(b("OH"), b("EE"), b("PD", 0, 128), GT)
        tt(b("HOH"), b("PA2", 0, 128), b("OH"), MUL)
        for a in range(16):
            mm(b("PB0", 0, 8), sel("SELh", a), b("HOH", a, 128, 16), a == 0, a == 15)
        mm(b("PA3", 0, 128), b("ID"), b(MWr, 0, 128))
        if not last:
            act(b("KOH"), b("OH"), AF.Copy, scale=col("pkf"))
            mm(b("PB1", 0, 8), b("ID"), b("base"), True, False)
        act(b("nh"), b("PC", 0, 128), AF.Relu, scale=-1.0, bias=1.0)
        act(b("hh"), b("PC", 0, 128), AF.Sign)
        if not last:
            tt(b("dx"), b(MWr, 256, 384), b("dsc"), MUL)
        cp(b(NLs), b("PB0", 0, 8))
        send("NL", t, s_rank, q_rank)

        tt(b("UN"), ind(b("X"), b(NLs)), b(MWr, 256, 384), NE)
        mm(b("PA0", 0, 128), b("BLK"), b("UN"))
        tt(b("UW"), b("PA3", 0, 128), b("UN"), MUL)
        mm(b("PA1", 0, 128), b("JM"), b("UW"))
        if not last:
            for a in range(16):
                mm(b("PB1", 0, 8), sel("SEL", a), b("KOH", a, 128, 16), False, a == 15)
            tt(b("TT"), ind(b("X"), b(NLs)), b("und"), MUL)
        tt(b("NF"), b("PA0", 0, 128), b(MWr, 128, 256), LE)
        tt(b(FSs), b("PA1", 0, 128), b("NF"), GT)
        send("FS", t, s_rank, q_rank)
        if not last:
            cp(b("SL"), b("PB1", 0, 8))
            win = ind(b("X"), b("SL"))
            op("V", lambda: g.vector.tensor_tensor(win[0], T.TT[:], T.dx[:], ADD),
               [("SL", 0, 8), ("TT", 0, 128), ("dx", 0, 128)], [("X", 0, 2048)])
        act(b("Fb"), b(FSs), AF.Copy, scale=32.0)
        mm(b("PD", 0, 128), b("IDh"), b("Cm"), True, False)
        tt(b("Hm"), b("Hf"), b("nh"), MUL)
        if last:
            tt(b("T2"), ind(b("As"), b(NLs)), b("hh"), MUL)
            tt(b("Hf"), b("T2"), b("Hm"), ADD)
            dma("Y", T.ycand[:], T.Hf[:], [("Hf", 0, 128)], [])
        tt(b("pre"), b("w32"), b("Fb"), MAX)
        if last:
            break

        tt(b("T1"), ind(b("As"), b(NLr)), b("mm"), MUL)
        mm(b("PD", 0, 128), b("IDh"), b("T1"), False, True)
        cp(b("Cu"), b("PD", 0, 128))
        for j in range(6 * t, min(16, 6 * t + 6)):
            act(sel("SELT", j), b("BLK"), AF.Copy, scale=col("KJ", j))

    for j in range(8):
        o = b("PA%d" % (2 + j // 4), j % 4 * 128, j % 4 * 128 + 128)
        mm(o, sel("SELT", 8 + j), b("pre"), True, False)
        mm(o, b("NI"), b("pre"), False, True)
        mm(b("PA%d" % (j // 4), j % 4 * 128, j % 4 * 128 + 128), sel("SELT", j), b("pre"))
    for j in range(4):
        cp(b("W4", 128 * j, 128 * j + 128), b("pre"))
    mm(b("PB1", 0, 128), b("BLK"), b(FSs))
    mm(b("PC", 0, 128), b("NB"), b(FSs), True, False)
    mm(b("PC", 0, 128), b("LC"), b("C512"), False, False)
    for i in range(2):
        act(b("NQ", 1024 + 512 * i, 1536 + 512 * i), b("PA%d" % (2 + i)), AF.Sign)
        tt(b("NQ", 512 * i, 512 * i + 512), b("PA%d" % i), b("W4"), GT)
        for k in range(4 * i, 4 * i + 4):
            mm(b("PC", 0, 128), b("ID"), b("NQ", 128 * k, 128 * k + 128), False, False)
            mm(b("PC", 0, 128), b("IH"), b("NQ", 1024 + 128 * k, 1152 + 128 * k), False, k == 7)
    act(b("e2"), b("PB1", 0, 128), AF.Copy)
    act(b("nF2"), b(FSs), AF.Identity, scale=-1.0, bias=1.0)
    act(b("Fb"), b(FSs), AF.Copy, scale=64.0)
    tt(b("T1"), ind(b("As"), b(NLr)), b("mm"), MUL)
    mm(b("PD", 0, 128), b("IDh"), b("T1"), False, True)
    act(b("Cf"), b("PD", 0, 128), AF.Copy)
    dma("Y", T.yctx[:], T.Cf[:], [("Cf", 0, 128)], [])
    tt(b("DD"), b("PC", 0, 128), b("nF2"), MUL)
    tt(b("qq"), b(FSr), b("DD"), MUL)
    mm(b("PB1", 0, 128), b("BLK"), b("qq"))
    mm(b("PB0", 0, 128), b("BLK"), b(FSr))
    tt(b("R4"), b("PC", 0, 128), b("Fb"), ADD)
    tt(b("R2"), b("PC", 0, 128), b("e2"), ADD)
    tt(b("bb"), b("R2"), b("qq"), SUB)
    tt(b("tq"), b("R4"), b("PB1", 0, 128), LT)
    tt(b("bb"), b("bb"), b("tq"), ADD)
    dma("Y", T.ypref[:], T.bb[:], [("bb", 0, 128)], [])
    tt(b("Rf"), b("PB0", 0, 128), b("Ai"), ADD)
    dma("S", T.yfail[:], T.Rf[0:128:16, :], [("Rf", 0, 128)], [])
    for sem in sorted(total):
        if known["Y"].get(sem, 0) < total[sem]:
            g.sync.wait_ge(T.sem[sem], total[sem])
